import numpy as np
import ml_dtypes


def mxq(x, axis, fmt="e4m3"):
    dtype, down = {"e4m3": (ml_dtypes.float8_e4m3fn, 7), "e5m2": (ml_dtypes.float8_e5m2, 14)}[fmt]
    v = np.moveaxis(np.asarray(x, np.float32).astype(ml_dtypes.bfloat16).astype(np.float64), axis, -1)
    blocks = v.reshape(v.shape[:-1] + (-1, 32))
    amax = np.abs(blocks).max(-1, keepdims=True)
    byte = np.maximum(np.where(amax > 0, np.frexp(amax)[1] - 1 + 127, 0) - down, 1)
    scale = np.exp2(byte - 127.0)
    codes = (blocks / scale).astype(np.float32).astype(dtype).astype(np.float64)
    return np.moveaxis((codes * scale).reshape(v.shape), -1, axis)


WIDE = False


def mx_kscale(k):
    if not WIDE:
        return np.ones(k)
    levels = np.array([10, -10, 5, -5, 0])
    if k % 512:
        return np.exp2(np.random.permutation(np.resize(levels, k // 32))).repeat(32)
    a = np.empty((k // 512, 16))
    for p in range(k // 512):
        a[p, :8] = np.random.permutation(np.resize(levels, 8))
        for g in range(8):
            far = levels[np.abs(levels - a[p, g]) >= 10]
            a[p, g + 8] = far[np.random.randint(len(far))]
    return np.exp2(a.ravel()).repeat(32)


def f64(x):
    return np.asarray(x).astype(np.float64)


def striped(idx):
    return np.tile(np.asarray(idx).reshape(-1, 16).T, (8, 1)).astype(np.uint16)


def unstriped(offs):
    return offs[:16].T.reshape(-1).astype(np.int64)


E2M1 = np.array([0.0, 0.5, 1.0, 1.5, 2.0, 3.0, 4.0, 6.0, -0.0, -0.5, -1.0, -1.5, -2.0, -3.0, -4.0, -6.0])


def pack_weight(w, fmt):
    k, n = w.shape
    w = f64(np.asarray(w, np.float32).astype(ml_dtypes.bfloat16)).reshape(k // 32, 32, n)
    amax = np.abs(w).max(1)
    if fmt == "e4m3":
        byte = np.frexp(amax)[1] - 1 + 127 - 7
    else:
        mant, ex = np.frexp(amax / 6.0)
        byte = np.where(mant > 0.5, ex, ex - 1) + 127
    byte = np.clip(np.where(amax > 0, byte, 1), 1, 254)
    scaled = (w * np.exp2(127.0 - byte)[:, None, :]).reshape(k, n).astype(np.float32)
    by_word = np.ascontiguousarray(scaled.reshape(k // 512, 128, 4, n).transpose(0, 1, 3, 2))
    if fmt == "e4m3":
        words = by_word.astype(ml_dtypes.float8_e4m3fn).view(np.uint8)
    else:
        c = by_word.astype(ml_dtypes.float4_e2m1fn).view(np.uint8) & 0xF
        words = (c[..., 0::2] | (c[..., 1::2] << 4)).reshape(k // 512, 128, 2 * n)
    return np.ascontiguousarray(words), np.ascontiguousarray(byte.astype(np.uint8).reshape(k // 512, 16, n))


def unpack_weight(words, scales, fmt):
    g, _, n = scales.shape
    words = np.ascontiguousarray(words).reshape(g, 128, n, -1)
    if fmt == "e4m3":
        vals = words.view(ml_dtypes.float8_e4m3fn).astype(np.float64)
    else:
        nib = np.empty((g, 128, n, 4), np.uint8)
        nib[..., 0::2] = words & 0xF
        nib[..., 1::2] = words >> 4
        vals = E2M1[nib]
    vals = vals * np.repeat(np.exp2(scales.astype(np.float64) - 127.0), 8, axis=1)[..., None]
    return vals.transpose(0, 1, 3, 2).reshape(g * 512, n)


C, I, T, L, N = 2048, 512, 512, 512, 512


def setup_inputs():
    n = np.random.standard_normal
    idx = np.random.permutation(C)[:I]
    fi = mx_kscale(I)
    fl = mx_kscale(L)
    ti = np.ones(C)
    ti[idx] = fi
    wp = pack_weight(n((I, N)) * 1 / np.sqrt(I) * fi[:, None], "e2m1")
    cxp = pack_weight(n((L, T)) / fl[:, None], "e4m3")
    wcp = pack_weight(n((L, N)) * 1 / np.sqrt(L) * fl[:, None], "e2m1")
    return {
        "xt": (n((T, C)) / ti).astype(np.float32),
        "w_words": wp[0],
        "w_scales": wp[1],
        "cx_words": cxp[0],
        "cx_scales": cxp[1],
        "wc_words": wcp[0],
        "wc_scales": wcp[1],
        "offs": striped(idx),
    }


def reference(xt, w_words, w_scales, cx_words, cx_scales, wc_words, wc_scales, offs):
    idx = unstriped(offs)
    wu = unpack_weight(w_words, w_scales, "e2m1")
    cxu = unpack_weight(cx_words, cx_scales, "e4m3")
    wcu = unpack_weight(wc_words, wc_scales, "e2m1")
    xs = f64(xt)[:, idx].T
    xsq = mxq(xs, 0, "e4m3")
    a1 = wu.T @ xsq
    b1 = wcu.T @ cxu
    y = np.maximum(a1, 0.0) * b1
    return y

@@ -1,0 +1,141 @@
+from contextlib import ExitStack
+
+import concourse.mybir as mybir
+from concourse.masks import make_identity
+
+C, I, T, L, N = 2048, 512, 512, 512, 512
+FLOPS = 2 * N * T * (I + L)
+
+F32 = mybir.dt.float32
+BF16 = mybir.dt.bfloat16
+I32 = mybir.dt.int32
+U32 = mybir.dt.uint32
+U16 = mybir.dt.uint16
+U8 = mybir.dt.uint8
+FP8X4 = mybir.dt.float8_e4m3fn_x4
+FP4X4 = mybir.dt.float4_e2m1fn_x4
+P = 128
+NT = N // P
+TT = T // P
+
+
+def tile_list_features_by_list_kernel(tc, xt, w_words, w_scales, cx_words, cx_scales, wc_words, wc_scales, offs, out):
+    nc = tc.nc
+    with ExitStack() as ctx:
+        keep = ctx.enter_context(tc.tile_pool(name="keep", bufs=1))
+        psum = ctx.enter_context(tc.psum_pool(name="psum", bufs=1))
+
+        offsets = keep.tile([P, I // 16], U16, name="offsets")
+        rows = [keep.tile([P, C], F32, name=f"rows{k}") for k in range(TT)]
+        w_sb = keep.tile([P, 2 * N], U8, name="w_sb", align_bytes=64)
+        wc_sb = keep.tile([P, 2 * N], U8, name="wc_sb", align_bytes=64)
+        cx_sb = keep.tile([P, T], U32, name="cx_sb", align_bytes=64)
+        staged = keep.tile([16, 3 * N], U8, name="staged", align_bytes=64)
+        planes = keep.tile([P, 3 * N], U8, name="planes", align_bytes=64)
+        ident = keep.tile([P, P], F32, name="ident")
+        b_sb = keep.tile([P, NT, T], F32, name="b_sb")
+
+        nc.vector.memset(planes[:].bitcast(I32), 0)
+        make_identity(nc, ident[:])
+
+        nc.sync.dma_start(offsets[:], offs)
+        for a, src in enumerate((w_scales, wc_scales, cx_scales)):
+            nc.sync.dma_start(staged[:, a * N : (a + 1) * N].bitcast(I32), src[0].bitcast(I32))
+        nc.sync.dma_start(rows[0][:], xt[0:P, :])
+        nc.sync.dma_start(w_sb[:].bitcast(I32), w_words[0].bitcast(I32))
+        nc.sync.dma_start(wc_sb[:].bitcast(I32), wc_words[0].bitcast(I32))
+        nc.sync.dma_start(cx_sb[:].bitcast(I32), cx_words[0].rearrange("p n t -> p (n t)").bitcast(I32))
+        nc.sync.dma_start(rows[1][:], xt[P : 2 * P, :])
+        for q in range(4):
+            nc.scalar.dma_start(planes[32 * q : 32 * q + 4, :].bitcast(I32), staged[4 * q : 4 * q + 4, :].bitcast(I32))
+        for k in range(2, TT):
+            nc.sync.dma_start(rows[k][:], xt[k * P : (k + 1) * P, :])
+
+        w_sc = planes[:, 0:N]
+        wc_sc = planes[:, N : 2 * N]
+        cx_sc = planes[:, 2 * N : 3 * N]
+
+        def context(j):
+            bank = psum.tile([P, T], F32, name=f"b_bank{j}")
+            nc.tensor.matmul_mx(
+                out=bank[:],
+                lhsT=wc_sb[:, 2 * P * j : 2 * P * (j + 1)].bitcast(FP4X4),
+                lhsT_scale=wc_sc[:, P * j : P * (j + 1)],
+                rhs=cx_sb[:].bitcast(FP8X4),
+                rhs_scale=cx_sc,
+                start=True,
+                stop=True,
+            )
+            nc.scalar.copy(b_sb[:, j, :], bank[:])
+
+        picked, grouped, codes, scales, sums = {}, {}, {}, {}, {}
+
+        def gather(k):
+            picked[k] = keep.tile([P, I], BF16, name=f"picked{k}", align_bytes=64)
+            nc.vector.tensor_copy(picked[k][:], rows[k][:].indirect(offsets[:]))
+            words = picked[k][:].bitcast(F32)
+            turned = psum.tile([P, 2, P], F32, name="turned", bufs=2)
+            for u in range(2):
+                nc.tensor.transpose(turned[:, u, :], words[:, u : I // 2 : 2], ident[:])
+            grouped[k] = keep.tile([P, 4 * P], BF16, name=f"grouped{k}", align_bytes=64)
+            nc.scalar.copy(
+                grouped[k][:].bitcast(F32).rearrange("p (r u) -> p r u", u=2),
+                turned[:].rearrange("p u r -> p r u"),
+            )
+
+        def product(k):
+            codes[k] = keep.tile([P, P], U32, name=f"codes{k}", align_bytes=64)
+            scales[k] = keep.tile([P, P], U8, name=f"scales{k}", align_bytes=64)
+            nc.vector.quantize_mx(out=codes[k][:].bitcast(FP8X4), scales=scales[k][:], in_=grouped[k][:])
+            for h in range(2):
+                sums[k, h] = psum.tile([P, 2, P], F32, name="a_bank", bufs=2)
+                for jj in range(2):
+                    j = 2 * h + jj
+                    nc.tensor.matmul_mx(
+                        out=sums[k, h][:, jj, :],
+                        lhsT=w_sb[:, 2 * P * j : 2 * P * (j + 1)].bitcast(FP4X4),
+                        lhsT_scale=w_sc[:, P * j : P * (j + 1)],
+                        rhs=codes[k][:].bitcast(FP8X4),
+                        rhs_scale=scales[k][:],
+                        start=True,
+                        stop=True,
+                    )
+
+        res01 = keep.tile([P, NT, 2 * P], F32, name="res01")
+        res2 = keep.tile([P, NT, P], F32, name="res2")
+        res3 = [keep.tile([P, 2, P], F32, name=f"res3_{h}") for h in range(2)]
+        out_v = out.rearrange("(j p) t -> p j t", p=P)
+
+        def finish(k):
+            for h in range(2):
+                if k < 2:
+                    dst = res01[:, 2 * h : 2 * h + 2, k * P : (k + 1) * P]
+                elif k == 2:
+                    dst = res2[:, 2 * h : 2 * h + 2, :]
+                else:
+                    dst = res3[h][:]
+                nc.vector.scalar_tensor_tensor(
+                    out=dst,
+                    in0=sums[k, h][:],
+                    scalar=0.0,
+                    in1=b_sb[:, 2 * h : 2 * h + 2, k * P : (k + 1) * P],
+                    op0=mybir.AluOpType.max,
+                    op1=mybir.AluOpType.mult,
+                )
+                if k == 3:
+                    eng = nc.scalar if h == 0 else nc.sync
+                    eng.dma_start(out_v[:, 2 * h : 2 * h + 2, k * P : (k + 1) * P], res3[h][:])
+            if k == 1:
+                nc.sync.dma_start(out_v[:, :, 0 : 2 * P], res01[:])
+            if k == 2:
+                nc.sync.dma_start(out_v[:, :, 2 * P : 3 * P], res2[:])
+
+        gather(0)
+        for j in range(NT):
+            context(j)
+        product(0)
+        for k in range(1, TT):
+            gather(k)
+            finish(k - 1)
+            product(k)
+        finish(TT - 1)

@@ -26,116 +26,127 @@ def tile_list_features_by_list_kernel(tc, xt, w_words, w_scales, cx_words, cx_sc
         psum = ctx.enter_context(tc.psum_pool(name="psum", bufs=1))
 
         offsets = keep.tile([P, I // 16], U16, name="offsets")
-        rows = [keep.tile([P, C], F32, name=f"rows{k}") for k in range(TT)]
         w_sb = keep.tile([P, 2 * N], U8, name="w_sb", align_bytes=64)
         wc_sb = keep.tile([P, 2 * N], U8, name="wc_sb", align_bytes=64)
         cx_sb = keep.tile([P, T], U32, name="cx_sb", align_bytes=64)
-        staged = keep.tile([16, 3 * N], U8, name="staged", align_bytes=64)
-        planes = keep.tile([P, 3 * N], U8, name="planes", align_bytes=64)
+        ctx_planes = keep.tile([P, N + T], U8, name="ctx_planes", align_bytes=64)
+        w_sc = keep.tile([P, N], U8, name="w_sc", align_bytes=64)
         ident = keep.tile([P, P], F32, name="ident")
-        b_sb = keep.tile([P, NT, T], F32, name="b_sb")
+        wc_sc = ctx_planes[:, 0:N]
+        cx_sc = ctx_planes[:, N : N + T]
 
-        nc.vector.memset(planes[:].bitcast(I32), 0)
-        make_identity(nc, ident[:])
+        nc.gpsimd.memset(ctx_planes[:].bitcast(I32), 0)
+        nc.gpsimd.memset(w_sc[:].bitcast(I32), 0)
+        nc.vector.memset(ident[:], 0.0)
+        make_identity(nc, ident[:], nomemset=True)
 
-        nc.sync.dma_start(offsets[:], offs)
-        for a, src in enumerate((w_scales, wc_scales, cx_scales)):
-            nc.sync.dma_start(staged[:, a * N : (a + 1) * N].bitcast(I32), src[0].bitcast(I32))
-        nc.sync.dma_start(rows[0][:], xt[0:P, :])
-        nc.sync.dma_start(w_sb[:].bitcast(I32), w_words[0].bitcast(I32))
-        nc.sync.dma_start(wc_sb[:].bitcast(I32), wc_words[0].bitcast(I32))
-        nc.sync.dma_start(cx_sb[:].bitcast(I32), cx_words[0].rearrange("p n t -> p (n t)").bitcast(I32))
-        nc.sync.dma_start(rows[1][:], xt[P : 2 * P, :])
-        for q in range(4):
-            nc.scalar.dma_start(planes[32 * q : 32 * q + 4, :].bitcast(I32), staged[4 * q : 4 * q + 4, :].bitcast(I32))
-        for k in range(2, TT):
+        rows = {}
+
+        def load_rows(k):
+            rows[k] = keep.tile([P, C], F32, name=f"rows{k}", tag=f"rows{k}", align_bytes=64)
             nc.sync.dma_start(rows[k][:], xt[k * P : (k + 1) * P, :])
 
-        w_sc = planes[:, 0:N]
-        wc_sc = planes[:, N : 2 * N]
-        cx_sc = planes[:, 2 * N : 3 * N]
+        def load_plane(queue, plane, src):
+            for q in range(4):
+                queue.dma_start(plane[32 * q : 32 * q + 4, :].bitcast(I32), src[0][4 * q : 4 * q + 4, :].bitcast(I32))
 
-        def context(j):
-            bank = psum.tile([P, T], F32, name=f"b_bank{j}")
-            nc.tensor.matmul_mx(
-                out=bank[:],
-                lhsT=wc_sb[:, 2 * P * j : 2 * P * (j + 1)].bitcast(FP4X4),
-                lhsT_scale=wc_sc[:, P * j : P * (j + 1)],
-                rhs=cx_sb[:].bitcast(FP8X4),
-                rhs_scale=cx_sc,
-                start=True,
-                stop=True,
-            )
-            nc.scalar.copy(b_sb[:, j, :], bank[:])
+        nc.sync.dma_start(offsets[:], offs)
+        nc.sync.dma_start(wc_sb[:].bitcast(I32), wc_words[0].bitcast(I32))
+        nc.sync.dma_start(cx_sb[:].bitcast(I32), cx_words[0].rearrange("p n t -> p (n t)").bitcast(I32))
+        load_plane(nc.sync, wc_sc, wc_scales)
+        load_rows(0)
+        load_plane(nc.sync, cx_sc, cx_scales)
+        nc.sync.dma_start(w_sb[:].bitcast(I32), w_words[0].bitcast(I32))
+        load_rows(1)
+        load_plane(nc.sync, w_sc[:], w_scales)
+        load_rows(2)
+        load_rows(3)
 
-        picked, grouped, codes, scales, sums = {}, {}, {}, {}, {}
+        grouped, codes, scales, sums = {}, {}, {}, {}
+
+        b_sb = keep.tile([P, NT, T], F32, name="b_sb")
+
+        def context():
+            for j in range(NT):
+                bank = psum.tile([P, T], F32, name=f"b_bank{j}", tag=f"bank{j}")
+                nc.tensor.matmul_mx(
+                    out=bank[:],
+                    lhsT=wc_sb[:, 2 * P * j : 2 * P * (j + 1)].bitcast(FP4X4),
+                    lhsT_scale=wc_sc[:, P * j : P * (j + 1)],
+                    rhs=cx_sb[:].bitcast(FP8X4),
+                    rhs_scale=cx_sc,
+                    start=True,
+                    stop=True,
+                )
+                nc.scalar.copy(b_sb[:, j, :], bank[:])
 
         def gather(k):
-            picked[k] = keep.tile([P, I], BF16, name=f"picked{k}", align_bytes=64)
-            nc.vector.tensor_copy(picked[k][:], rows[k][:].indirect(offsets[:]))
-            words = picked[k][:].bitcast(F32)
-            turned = psum.tile([P, 2, P], F32, name="turned", bufs=2)
+            picked = keep.tile([P, I], BF16, name=f"picked{k}", tag=f"picked{k}", align_bytes=64)
+            nc.vector.tensor_copy(picked[:], rows[k][:].indirect(offsets[:]))
+            words = picked[:].bitcast(F32)
+            turned = psum.tile([P, 2, P], F32, name=f"turned{k}", tag=f"bank{4 + k % 2}")
             for u in range(2):
                 nc.tensor.transpose(turned[:, u, :], words[:, u : I // 2 : 2], ident[:])
-            grouped[k] = keep.tile([P, 4 * P], BF16, name=f"grouped{k}", align_bytes=64)
+            grouped[k] = keep.tile([P, 4 * P], BF16, name=f"grouped{k}", tag=f"grouped{k}", align_bytes=64)
             nc.scalar.copy(
                 grouped[k][:].bitcast(F32).rearrange("p (r u) -> p r u", u=2),
                 turned[:].rearrange("p u r -> p r u"),
             )
 
-        def product(k):
-            codes[k] = keep.tile([P, P], U32, name=f"codes{k}", align_bytes=64)
+        def quantise(k):
+            codes[k] = keep.tile([P, P], U32, name=f"codes{k}", tag=f"rows{k + 1}", align_bytes=64)[:]
             scales[k] = keep.tile([P, P], U8, name=f"scales{k}", align_bytes=64)
-            nc.vector.quantize_mx(out=codes[k][:].bitcast(FP8X4), scales=scales[k][:], in_=grouped[k][:])
-            for h in range(2):
-                sums[k, h] = psum.tile([P, 2, P], F32, name="a_bank", bufs=2)
-                for jj in range(2):
-                    j = 2 * h + jj
+            nc.vector.quantize_mx(out=codes[k].bitcast(FP8X4), scales=scales[k][:], in_=grouped[k][:])
+
+        def product(k):
+            parts = 2 if k == TT - 1 else 1
+            width = NT // parts
+            for h in range(parts):
+                tag = f"bank{h}" if parts == 2 else f"bank{6 + k % 2}"
+                sums[k, h] = psum.tile([P, width, P], F32, name=f"a_bank{k}_{h}", tag=tag)
+                for jj in range(width):
+                    j = width * h + jj
                     nc.tensor.matmul_mx(
                         out=sums[k, h][:, jj, :],
                         lhsT=w_sb[:, 2 * P * j : 2 * P * (j + 1)].bitcast(FP4X4),
                         lhsT_scale=w_sc[:, P * j : P * (j + 1)],
-                        rhs=codes[k][:].bitcast(FP8X4),
+                        rhs=codes[k].bitcast(FP8X4),
                         rhs_scale=scales[k][:],
                         start=True,
                         stop=True,
                     )
 
-        res01 = keep.tile([P, NT, 2 * P], F32, name="res01")
-        res2 = keep.tile([P, NT, P], F32, name="res2")
-        res3 = [keep.tile([P, 2, P], F32, name=f"res3_{h}") for h in range(2)]
         out_v = out.rearrange("(j p) t -> p j t", p=P)
 
         def finish(k):
-            for h in range(2):
-                if k < 2:
-                    dst = res01[:, 2 * h : 2 * h + 2, k * P : (k + 1) * P]
-                elif k == 2:
-                    dst = res2[:, 2 * h : 2 * h + 2, :]
-                else:
-                    dst = res3[h][:]
+            last = k == TT - 1
+            res = keep.tile([P, NT, P], F32, name=f"res{k}", tag=f"grouped{k + 1}", align_bytes=64)
+            parts = 2 if last else 1
+            width = NT // parts
+            for h in range(parts):
+                js = slice(width * h, width * (h + 1))
                 nc.vector.scalar_tensor_tensor(
-                    out=dst,
+                    out=res[:, js, :],
                     in0=sums[k, h][:],
                     scalar=0.0,
-                    in1=b_sb[:, 2 * h : 2 * h + 2, k * P : (k + 1) * P],
+                    in1=b_sb[:, js, k * P : (k + 1) * P],
                     op0=mybir.AluOpType.max,
                     op1=mybir.AluOpType.mult,
                 )
-                if k == 3:
-                    eng = nc.scalar if h == 0 else nc.sync
-                    eng.dma_start(out_v[:, 2 * h : 2 * h + 2, k * P : (k + 1) * P], res3[h][:])
-            if k == 1:
-                nc.sync.dma_start(out_v[:, :, 0 : 2 * P], res01[:])
-            if k == 2:
-                nc.sync.dma_start(out_v[:, :, 2 * P : 3 * P], res2[:])
+                if last:
+                    (nc.scalar, nc.sync)[h].dma_start(out_v[:, js, k * P : (k + 1) * P], res[:, js, :])
+            if not last:
+                nc.sync.dma_start(out_v[:, :, k * P : (k + 1) * P], res[:, :, :])
 
         gather(0)
-        for j in range(NT):
-            context(j)
-        product(0)
+        context()
         for k in range(1, TT):
             gather(k)
-            finish(k - 1)
-            product(k)
+            quantise(k - 1)
+            product(k - 1)
+            if k > 1:
+                finish(k - 2)
+        quantise(TT - 1)
+        product(TT - 1)
+        finish(TT - 2)
         finish(TT - 1)

from contextlib import ExitStack

import concourse.mybir as mybir
from concourse.masks import make_identity

C, I, T, L, N = 2048, 512, 512, 512, 512
FLOPS = 2 * N * T * (I + L)

F32 = mybir.dt.float32
BF16 = mybir.dt.bfloat16
I32 = mybir.dt.int32
U32 = mybir.dt.uint32
U16 = mybir.dt.uint16
U8 = mybir.dt.uint8
FP8X4 = mybir.dt.float8_e4m3fn_x4
FP4X4 = mybir.dt.float4_e2m1fn_x4
P = 128
NT = N // P
TT = T // P


def tile_list_features_by_list_kernel(tc, xt, w_words, w_scales, cx_words, cx_scales, wc_words, wc_scales, offs, out):
    nc = tc.nc
    with ExitStack() as ctx:
        keep = ctx.enter_context(tc.tile_pool(name="keep", bufs=1))
        psum = ctx.enter_context(tc.psum_pool(name="psum", bufs=1))

        offsets = keep.tile([P, I // 16], U16, name="offsets")
        w_sb = keep.tile([P, 2 * N], U8, name="w_sb", align_bytes=64)
        wc_sb = keep.tile([P, 2 * N], U8, name="wc_sb", align_bytes=64)
        cx_sb = keep.tile([P, T], U32, name="cx_sb", align_bytes=64)
        ctx_planes = keep.tile([P, N + T], U8, name="ctx_planes", align_bytes=64)
        w_sc = keep.tile([P, N], U8, name="w_sc", align_bytes=64)
        ident = keep.tile([P, P], F32, name="ident")
        wc_sc = ctx_planes[:, 0:N]
        cx_sc = ctx_planes[:, N : N + T]

        nc.gpsimd.memset(ctx_planes[:].bitcast(I32), 0)
        nc.gpsimd.memset(w_sc[:].bitcast(I32), 0)
        nc.vector.memset(ident[:], 0.0)
        make_identity(nc, ident[:], nomemset=True)

        rows = {}

        def load_rows(k):
            rows[k] = keep.tile([P, C], F32, name=f"rows{k}", tag=f"rows{k}", align_bytes=64)
            nc.sync.dma_start(rows[k][:], xt[k * P : (k + 1) * P, :])

        def load_plane(queue, plane, src):
            for q in range(4):
                queue.dma_start(plane[32 * q : 32 * q + 4, :].bitcast(I32), src[0][4 * q : 4 * q + 4, :].bitcast(I32))

        nc.sync.dma_start(offsets[:], offs)
        nc.sync.dma_start(wc_sb[:].bitcast(I32), wc_words[0].bitcast(I32))
        nc.sync.dma_start(cx_sb[:].bitcast(I32), cx_words[0].rearrange("p n t -> p (n t)").bitcast(I32))
        load_plane(nc.sync, wc_sc, wc_scales)
        load_rows(0)
        load_plane(nc.sync, cx_sc, cx_scales)
        nc.sync.dma_start(w_sb[:].bitcast(I32), w_words[0].bitcast(I32))
        load_rows(1)
        load_plane(nc.sync, w_sc[:], w_scales)
        load_rows(2)
        load_rows(3)

        grouped, codes, scales, sums = {}, {}, {}, {}

        b_sb = keep.tile([P, NT, T], F32, name="b_sb")

        def context():
            for j in range(NT):
                bank = psum.tile([P, T], F32, name=f"b_bank{j}", tag=f"bank{j}")
                nc.tensor.matmul_mx(
                    out=bank[:],
                    lhsT=wc_sb[:, 2 * P * j : 2 * P * (j + 1)].bitcast(FP4X4),
                    lhsT_scale=wc_sc[:, P * j : P * (j + 1)],
                    rhs=cx_sb[:].bitcast(FP8X4),
                    rhs_scale=cx_sc,
                    start=True,
                    stop=True,
                )
                nc.scalar.copy(b_sb[:, j, :], bank[:])

        def gather(k):
            picked = keep.tile([P, I], BF16, name=f"picked{k}", tag=f"picked{k}", align_bytes=64)
            nc.vector.tensor_copy(picked[:], rows[k][:].indirect(offsets[:]))
            words = picked[:].bitcast(F32)
            turned = psum.tile([P, 2, P], F32, name=f"turned{k}", tag=f"bank{4 + k % 2}")
            for u in range(2):
                nc.tensor.transpose(turned[:, u, :], words[:, u : I // 2 : 2], ident[:])
            grouped[k] = keep.tile([P, 4 * P], BF16, name=f"grouped{k}", tag=f"grouped{k}", align_bytes=64)
            nc.scalar.copy(
                grouped[k][:].bitcast(F32).rearrange("p (r u) -> p r u", u=2),
                turned[:].rearrange("p u r -> p r u"),
            )

        def quantise(k):
            codes[k] = keep.tile([P, P], U32, name=f"codes{k}", tag=f"rows{k + 1}", align_bytes=64)[:]
            scales[k] = keep.tile([P, P], U8, name=f"scales{k}", align_bytes=64)
            nc.vector.quantize_mx(out=codes[k].bitcast(FP8X4), scales=scales[k][:], in_=grouped[k][:])

        def product(k):
            parts = 2 if k == TT - 1 else 1
            width = NT // parts
            for h in range(parts):
                tag = f"bank{h}" if parts == 2 else f"bank{6 + k % 2}"
                sums[k, h] = psum.tile([P, width, P], F32, name=f"a_bank{k}_{h}", tag=tag)
                for jj in range(width):
                    j = width * h + jj
                    nc.tensor.matmul_mx(
                        out=sums[k, h][:, jj, :],
                        lhsT=w_sb[:, 2 * P * j : 2 * P * (j + 1)].bitcast(FP4X4),
                        lhsT_scale=w_sc[:, P * j : P * (j + 1)],
                        rhs=codes[k].bitcast(FP8X4),
                        rhs_scale=scales[k][:],
                        start=True,
                        stop=True,
                    )

        out_v = out.rearrange("(j p) t -> p j t", p=P)

        def finish(k):
            last = k == TT - 1
            res = keep.tile([P, NT, P], F32, name=f"res{k}", tag=f"grouped{k + 1}", align_bytes=64)
            parts = 2 if last else 1
            width = NT // parts
            for h in range(parts):
                js = slice(width * h, width * (h + 1))
                nc.vector.scalar_tensor_tensor(
                    out=res[:, js, :],
                    in0=sums[k, h][:],
                    scalar=0.0,
                    in1=b_sb[:, js, k * P : (k + 1) * P],
                    op0=mybir.AluOpType.max,
                    op1=mybir.AluOpType.mult,
                )
                if last:
                    (nc.scalar, nc.sync)[h].dma_start(out_v[:, js, k * P : (k + 1) * P], res[:, js, :])
            if not last:
                nc.sync.dma_start(out_v[:, :, k * P : (k + 1) * P], res[:, :, :])

        gather(0)
        context()
        for k in range(1, TT):
            gather(k)
            quantise(k - 1)
            product(k - 1)
            if k > 1:
                finish(k - 2)
        quantise(TT - 1)
        product(TT - 1)
        finish(TT - 2)
        finish(TT - 1)
